import numpy as np
import ml_dtypes


def mxq(x, axis, fmt="e4m3"):
    dtype, down = {"e4m3": (ml_dtypes.float8_e4m3fn, 7), "e5m2": (ml_dtypes.float8_e5m2, 14)}[fmt]
    v = np.moveaxis(np.asarray(x, np.float32).astype(ml_dtypes.bfloat16).astype(np.float64), axis, -1)
    blocks = v.reshape(v.shape[:-1] + (-1, 32))
    amax = np.abs(blocks).max(-1, keepdims=True)
    byte = np.maximum(np.where(amax > 0, np.frexp(amax)[1] - 1 + 127, 0) - down, 1)
    scale = np.exp2(byte - 127.0)
    codes = (blocks / scale).astype(np.float32).astype(dtype).astype(np.float64)
    return np.moveaxis((codes * scale).reshape(v.shape), -1, axis)


WIDE = False


def mx_kscale(k):
    if not WIDE:
        return np.ones(k)
    levels = np.array([10, -10, 5, -5, 0])
    if k % 512:
        return np.exp2(np.random.permutation(np.resize(levels, k // 32))).repeat(32)
    a = np.empty((k // 512, 16))
    for p in range(k // 512):
        a[p, :8] = np.random.permutation(np.resize(levels, 8))
        for g in range(8):
            far = levels[np.abs(levels - a[p, g]) >= 10]
            a[p, g + 8] = far[np.random.randint(len(far))]
    return np.exp2(a.ravel()).repeat(32)


BF16 = ml_dtypes.bfloat16


def bf(x):
    return np.asarray(x, np.float32).astype(BF16)


def f64(x):
    return np.asarray(x).astype(np.float64)


E2M1 = np.array([0.0, 0.5, 1.0, 1.5, 2.0, 3.0, 4.0, 6.0, -0.0, -0.5, -1.0, -1.5, -2.0, -3.0, -4.0, -6.0])


def pack_weight(w, fmt):
    k, n = w.shape
    w = f64(bf(w)).reshape(k // 32, 32, n)
    amax = np.abs(w).max(1)
    if fmt == "e4m3":
        byte = np.frexp(amax)[1] - 1 + 127 - 7
    else:
        mant, ex = np.frexp(amax / 6.0)
        byte = np.where(mant > 0.5, ex, ex - 1) + 127
    byte = np.clip(np.where(amax > 0, byte, 1), 1, 254)
    scaled = (w * np.exp2(127.0 - byte)[:, None, :]).reshape(k, n).astype(np.float32)
    by_word = np.ascontiguousarray(scaled.reshape(k // 512, 128, 4, n).transpose(0, 1, 3, 2))
    if fmt == "e4m3":
        words = by_word.astype(ml_dtypes.float8_e4m3fn).view(np.uint8)
    else:
        c = by_word.astype(ml_dtypes.float4_e2m1fn).view(np.uint8) & 0xF
        words = c[..., 0::2] | (c[..., 1::2] << 4)
    return np.ascontiguousarray(words), np.ascontiguousarray(byte.astype(np.uint8).reshape(k // 512, 16, n))


def unpack_weight(words, scales, fmt):
    g, p, n, _ = words.shape
    if fmt == "e4m3":
        vals = np.ascontiguousarray(words).view(ml_dtypes.float8_e4m3fn).astype(np.float64)
    else:
        nib = np.empty((g, p, n, 4), np.uint8)
        nib[..., 0::2] = words & 0xF
        nib[..., 1::2] = words >> 4
        vals = E2M1[nib]
    vals = vals * np.repeat(np.exp2(scales.astype(np.float64) - 127.0), 8, axis=1)[..., None]
    return vals.transpose(0, 1, 3, 2).reshape(g * 512, n)
def pack4(w):
    words, scales = pack_weight(w, "e2m1")
    return words.reshape(words.shape[0], 128, -1), scales


def unpack4(words, scales):
    return unpack_weight(words.reshape(words.shape[0], 128, -1, 2), scales, "e2m1")


def planes(Y):
    n, m = Y.shape
    b = f64(bf(Y)).reshape(n // 32, 32, m)
    amax = np.abs(b).max(1)
    byte = np.clip(np.where(amax > 0, np.frexp(amax)[1] - 1 + 127 - 7, 1), 1, 254)
    codes = (b * np.exp2(127.0 - byte)[:, None, :]).reshape(n, m).astype(np.float32).astype(ml_dtypes.float8_e4m3fn).view(np.uint8)
    words = codes.reshape(n // 512, 128, 4, m).transpose(0, 1, 3, 2)
    return np.ascontiguousarray(words), np.ascontiguousarray(byte.astype(np.uint8).reshape(n // 512, 16, m))


N, M, K, L = 1024, 1024, 512, 1024


def positive_root(s, m):
    return 0.5 * (np.sqrt(s * s + 4.0 * m) - s)


def setup_inputs():
    s = mx_kscale(K)
    u = mx_kscale(N)
    r = np.random.uniform(0.5, 1.3, (N, 1))
    x = bf(np.random.standard_normal((N, K)) * r * s)
    beta = np.random.standard_normal((M, K)) * (1.2 / np.sqrt(K)) / s
    beta_words, beta_scales = pack4(beta.T)
    return {
        "x": x,
        "beta_words": beta_words,
        "beta_scales": beta_scales,
        "bs": bf(np.random.uniform(0.5, 1.5, M)),
        "mass": bf(np.random.uniform(0.5, 2.0, N)),
        "obs": bf(np.random.uniform(0.0, 1.6, (N, M))),
        "wt": bf((1.0 + 0.1 * np.random.standard_normal(N)) * u),
        "z": bf(np.random.standard_normal((N, L)) / np.sqrt(N) / u[:, None]),
    }


def core(x, beta_words, beta_scales, bs, mass, obs, wt, z):
    phi = mxq(f64(x), 1, "e4m3") @ unpack4(beta_words, beta_scales)
    e = f64(bs)[None, :] * np.exp(0.5 * phi)
    sn = np.mean(e, axis=1)
    a = positive_root(sn, f64(mass))
    fit = a[:, None] * e
    res = f64(wt)[:, None] * (f64(obs) - fit)
    return mxq(f64(z), 0, "e4m3").T @ mxq(res, 0, "e4m3")


def reference(x, beta_words, beta_scales, bs, mass, obs, wt, z):
    R_out = core(x, beta_words, beta_scales, bs, mass, obs, wt, z)
    words, scales = planes(R_out)
    return R_out, words, scales

from contextlib import ExitStack

import concourse.mybir as mybir
from concourse.masks import make_identity

N, M, K, L = 1024, 1024, 512, 1024
FLOPS = 2 * N * M * K + 2 * N * M * L

F32 = mybir.dt.float32
BF16 = mybir.dt.bfloat16
I32 = mybir.dt.int32
U32 = mybir.dt.uint32
U8 = mybir.dt.uint8
FP8X4 = mybir.dt.float8_e4m3fn_x4
FP4X4 = mybir.dt.float4_e2m1fn_x4
ALU = mybir.AluOpType
FUNC = mybir.ActivationFunctionType

P = 128
PACK = 4
BANK = 512
PAIR = 2 * P
TILES = 8

X_PIECES = [(0, 1), (1, 2), (2, 4), (4, 6), (6, 8)]
X_LOADS = [(0, 2), (2, 4), (4, 8)]

BS_BANK = 0
TURN_BANKS = [1, 2, 7, 1, 2]
WOBS_BANKS = [1, 2, 7, 0]
RING_BANKS = [3, 4, 5, 6]

ORDER = """
clear loadx0 loadwt loadx1 loadz01 zero loadbeta loadscale0 loadscale1 identity loadscale2 turn0 loadscale3 unit
loadbs loadmass loadz00 loadx2 turn1 loadz10 xpack0.v turn2 xquant0 zpack011.s xpack1.s zpack010.v loadobs0 diag
phi01 xpack2.s phi00 xquant1 zpack000.v expo01 phi11 terms phi10 expo00 spread zquant01 expo11 turn3 xquant2 expo10
phi20 zpack100.g xpack3.s phi31 phi21 rowsum0 phi30 rowsum1 expo20 turn4 expo21 wobs00 xquant3 expo31 rowsum2 expo30
loadz11 zpack101.g phi40 disc0.s phi51 loadobs1 disc1.s xpack4.s phi50 rowsum3 disc2.s expo51 phi41 wobs10 xquant4
expo50 disc3.s phi71 expo40 phi70 root04 expo41 zquant10 phi60 expo71 expo70 rowsum5 phi61 rowsum4 gap04 wobs01
factor04 disc5.s expo60 rowsum7 scale20.g expo61 scale30.v disc4.s scale10.s root46 rowsum6 scale00.s disc7.g
scale11.s resid10 gap46 disc6.g zpack111.s factor46 scale50.s wobs11 wobs30 root67 root78 factor67 resid00 wobs20
resid30 resid20 scale40.s factor78 scale70.s rquant00 wobs50 scale60.g zpack110.s scale41.g resid01 wobs40 resid11
wobs21 zpack001.s zquant11 wobs31 rquant01 resid21 scale61.s zquant00 moment10 scale31.s resid31 scale71.s moment11
wobs41 moment00 scale01.v drain10.s moment01 rquant11 scale21.v drain11.s rquant10 scale51.s resid50 roundcopy11.g
moment13 drain00.s resid40 wobs51 drain01.s moment12 resid41 roundbank13.s moment02 store10 store00 drain13.s wobs70
moment03 resid51 roundcopy10.g drain12.v roundbank12.s rquant21 wobs71 store11 rquant20 drain02.s wobs60 drain03.s
oquant11 wobs61 moment14 resid70 roundbank03.s resid60 moment15 roundcopy02.g store01 resid61 oquant01 drain14.s
moment05 drain15.s resid71 moment04 storecodes1 store12 drain05.s rquant30 drain04.s rquant31 roundcopy01.v
roundbank05.s store02 roundcopy00.v roundbank04.s oquant10 moment16 roundcopy14.v oquant00 moment17 drain16.s
moment07 drain17.s moment06 roundcopy15.v storecodes0 oquant02 roundbank16.s oquant12 store13 roundcopy17.v
roundbank07.s roundbank06.v storecodes2 drain06.s oquant13 oquant03 drain07.s storegroup13 storescales0.s
storescales3.y storescales2.s storescales1.y store03 storegroup03
"""


def tile_choosiowhalfsweepinstrumentmoments_x2_kernel(
    tc, x, beta_words, beta_scales, bs, mass, obs, wt, z, out_0, out_1, out_2
):
    nc = tc.nc
    x_rows = x.rearrange("(g p t) k -> g p t k", g=2, t=PACK)
    z_rows = z.rearrange("(g p t) l -> g p t l", g=2, t=PACK)
    obs_rows = obs.rearrange("(g p t) m -> g p t m", g=2, t=PACK)
    out_rows = out_0.rearrange("(h p t) m -> h p t m", h=2, t=PACK)
    out_words = out_1.rearrange("h p m t -> p h (m t)")

    with ExitStack() as ctx:
        keep = ctx.enter_context(tc.tile_pool(name="keep", bufs=1))
        roll = ctx.enter_context(tc.tile_pool(name="roll", bufs=4))
        psum = ctx.enter_context(tc.psum_pool(name="psum", bufs=1))
        ctx.enter_context(tc.manual_schedule())
        made = {}

        def sbuf(key, shape, dtype):
            if key not in made:
                made[key] = keep.tile(shape, dtype, name="".join(map(str, key)), align_bytes=64)
            return made[key]

        def new_bank(key, number, shape, dtype):
            made[key] = psum.tile(shape, dtype, name="".join(map(str, key)), tag="bank%d" % number)
            return made[key]

        def copy(engine, out, in_):
            if engine == "s":
                nc.scalar.copy(out=out, in_=in_)
            elif engine == "v":
                nc.vector.tensor_copy(out=out, in_=in_)
            else:
                nc.gpsimd.tensor_scalar(out=out, in0=in_, scalar1=1.0, scalar2=0.0, op0=ALU.mult, op1=ALU.add)

        def quantise(key, grouped):
            words = grouped.shape[1] // PACK
            codes = sbuf(key + ("codes",), [P, words], U32)
            scales = sbuf(key + ("scales",), [P, words], U8)
            nc.vector.quantize_mx(out=codes[:].bitcast(FP8X4), scales=scales[:], in_=grouped[:])

        def operand(key, cols):
            return made[key + ("codes",)][:, cols].bitcast(FP8X4), made[key + ("scales",)][:, cols]

        ident = sbuf(("ident",), [P, P], F32)
        ones = sbuf(("ones",), [P, P], BF16)
        bs_row = sbuf(("bs_row",), [P, M], BF16)
        half = sbuf(("half",), [P, TILES], F32)
        beta_codes = sbuf(("beta_codes",), [P, 2 * M], U8)
        beta_scale = sbuf(("beta_scale",), [P, M], U8)
        x_raw = [sbuf(("x_raw", i), [P, end - first, K], BF16) for i, (first, end) in enumerate(X_LOADS)]
        z_raw = {(g, h): sbuf(("z_raw", g, h), [P, PACK, BANK], BF16) for g in range(2) for h in range(2)}
        obs_raw = [sbuf(("obs_raw", g), [P, PACK, M], BF16) for g in range(2)]
        wt_col = sbuf(("wt_col",), [P, 2, PACK], BF16)
        mass_col = sbuf(("mass_col",), [P, 2, PACK], BF16)
        mass_term = sbuf(("mass_term",), [P, TILES], F32)
        wt_term = sbuf(("wt_term",), [P, TILES], F32)
        wt_diag = sbuf(("wt_diag",), [P, TILES, P], BF16)
        sums = sbuf(("sums",), [P, TILES], F32)
        disc_scalar = sbuf(("disc_scalar",), [P, TILES], F32)
        out_codes = sbuf(("out_codes",), [P, 2, M], U32)
        out_scales = sbuf(("out_scales",), [P, 2, M], U8)
        e = [sbuf(("e", g), [P, PACK, M], F32) for g in range(2)]

        def clear():
            nc.vector.memset(beta_scale[:].bitcast(I32), 0)
            nc.vector.memset(half[:], 0.5)

        def zero():
            nc.vector.memset(bs_row[:].bitcast(I32), 0)

        def identity():
            make_identity(nc, ident[:])

        def unit():
            nc.scalar.activation(out=ones[:], in_=ident[:], func=FUNC.Exp, scale=0.0)

        def loadx(i):
            first, end = X_LOADS[i]
            t = first % PACK
            nc.sync.dma_start(out=x_raw[i][:], in_=x_rows[first // PACK, :, t : t + end - first, :])

        def loadbeta():
            nc.sync.dma_start(out=beta_codes[:].bitcast(I32), in_=beta_words[0].bitcast(I32))

        def loadscale(d):
            nc.scalar.dma_start(
                out=beta_scale[32 * d : 32 * d + 4, :].bitcast(I32),
                in_=beta_scales[0, 4 * d : 4 * d + 4, :].bitcast(I32),
            )

        def loadwt():
            nc.gpsimd.dma_start(out=wt_col[:], in_=wt.rearrange("(g p t) -> p g t", g=2, t=PACK))

        def loadmass():
            nc.gpsimd.dma_start(out=mass_col[:], in_=mass.rearrange("(g p t) -> p g t", g=2, t=PACK))

        def loadbs():
            nc.gpsimd.dma_start(out=bs_row[0:1, :], in_=bs.rearrange("(o m) -> o m", o=1))

        def loadz(g, h):
            nc.sync.dma_start(out=z_raw[g, h][:], in_=z_rows[g, :, :, BANK * h : BANK * (h + 1)])

        def loadobs(g):
            nc.sync.dma_start(out=obs_raw[g][:], in_=obs_rows[g])

        def diag():
            for j in range(TILES):
                g, t = divmod(j, PACK)
                nc.vector.tensor_scalar(
                    out=wt_diag[:, j, :], in0=ident[:], scalar1=wt_col[:, g, t : t + 1], scalar2=None, op0=ALU.mult
                )

        def terms():
            for term, col, constant in ((mass_term, mass_col, 4.0 * M * M), (wt_term, wt_col, -0.5 / M)):
                nc.gpsimd.tensor_scalar(
                    out=term[:],
                    in0=col[:].rearrange("p g t -> p (g t)"),
                    scalar1=constant,
                    scalar2=0.0,
                    op0=ALU.mult,
                    op1=ALU.add,
                )

        def spread():
            bank = new_bank(("bs",), BS_BANK, [P, M], BF16)
            for f in range(2):
                cols = slice(BANK * f, BANK * (f + 1))
                nc.tensor.matmul(out=bank[:, cols], lhsT=ones[:], rhs=bs_row[:, cols], start=True, stop=True)

        def turn(u):
            first, end = X_PIECES[u]
            bank = new_bank(("turned", u), TURN_BANKS[u], [P, end - first, 2, P], F32)
            for j in range(first, end):
                i = max(i for i in range(len(X_LOADS)) if X_LOADS[i][0] <= j)
                pairs = x_raw[i][:, j - X_LOADS[i][0], :].bitcast(F32)
                for w in range(2):
                    nc.tensor.transpose(out=bank[:, j - first, w, :], in_=pairs[:, w : K // 2 : 2], identity=ident[:])

        def xpack(u, engine):
            first, end = X_PIECES[u]
            grouped = sbuf(("x_grouped", u), [P, K * (end - first)], BF16)
            copy(
                engine,
                grouped[:].bitcast(F32).rearrange("p (j r w) -> p j r w", j=end - first, w=2),
                made["turned", u][:].rearrange("p j w r -> p j r w"),
            )

        def xquant(u):
            quantise(("x", u), made["x_grouped", u])

        def phi(j, f):
            u = max(u for u in range(len(X_PIECES)) if X_PIECES[u][0] <= j)
            place = j - X_PIECES[u][0]
            codes, scales = operand(("x", u), slice(P * place, P * (place + 1)))
            bank = new_bank(("phi", j, f), RING_BANKS[(2 * j + f) % 4], [P, BANK], F32)
            nc.tensor.matmul_mx(
                out=bank[:],
                lhsT=codes,
                lhsT_scale=scales,
                rhs=beta_codes[:, 2 * BANK * f : 2 * BANK * (f + 1)].bitcast(FP4X4),
                rhs_scale=beta_scale[:, BANK * f : BANK * (f + 1)],
                start=True,
                stop=True,
            )

        def expo(j, f):
            if ("exp", j) not in made:
                made["exp", j] = roll.tile([P, M], F32, name="exp")
            nc.scalar.activation(
                out=made["exp", j][:, BANK * f : BANK * (f + 1)], in_=made["phi", j, f][:], func=FUNC.Exp, scale=0.5
            )

        def rowsum(j):
            nc.vector.scalar_tensor_tensor(
                out=e[j // PACK][:, j % PACK, :],
                in0=made["exp", j][:],
                scalar=1.0,
                in1=made["bs",][:],
                op0=ALU.mult,
                op1=ALU.mult,
                accum_out=sums[:, j : j + 1],
            )

        def disc(j, engine):
            col = slice(j, j + 1)
            if engine == "s":
                nc.scalar.activation(
                    out=disc_scalar[:, col], in_=sums[:, col], func=FUNC.Identity, scale=sums[:, col], bias=mass_term[:, col]
                )
            else:
                nc.gpsimd.tensor_scalar(
                    out=sbuf(("disc", j), [P, 1], F32)[:],
                    in0=sums[:, col],
                    scalar1=sums[:, col],
                    scalar2=mass_term[:, col],
                    op0=ALU.mult,
                    op1=ALU.add,
                )

        def root(first, end):
            source = made["disc", first][:] if ("disc", first) in made else disc_scalar[:, first:end]
            target = sbuf(("root", first), [P, end - first], F32)
            nc.gpsimd.tensor_tensor(out=target[:], in0=source, in1=half[:, first:end], op=ALU.pow)

        def gap(first, end):
            target = sbuf(("gap", first), [P, end - first], F32)
            nc.gpsimd.tensor_tensor(out=target[:], in0=made["root", first][:], in1=sums[:, first:end], op=ALU.subtract)

        def factor(first, end):
            target = sbuf(("factors", first), [P, end - first], F32)
            if end - first > 1:
                nc.gpsimd.tensor_tensor(out=target[:], in0=made["gap", first][:], in1=wt_term[:, first:end], op=ALU.mult)
            else:
                nc.gpsimd.tensor_scalar(
                    out=target[:],
                    in0=made["root", first][:],
                    scalar1=sums[:, first:end],
                    scalar2=wt_term[:, first:end],
                    op0=ALU.subtract,
                    op1=ALU.mult,
                )
            for j in range(first, end):
                made["factor", j] = target[:, j - first : j - first + 1]

        def scale(j, f, engine):
            part = e[j // PACK][:, j % PACK, BANK * f : BANK * (f + 1)]
            if engine == "s":
                nc.scalar.activation(out=part, in_=part, func=FUNC.Copy, scale=made["factor", j])
            elif engine == "v":
                nc.vector.tensor_scalar(out=part, in0=part, scalar1=made["factor", j], scalar2=None, op0=ALU.mult)
            else:
                nc.gpsimd.tensor_scalar(
                    out=part, in0=part, scalar1=made["factor", j], scalar2=0.0, op0=ALU.mult, op1=ALU.add
                )

        def zpack(g, h, c, engine):
            grouped = sbuf(("z_grouped", g, h), [P, PACK * BANK], BF16)
            places = slice(P // 2 * c, P // 2 * (c + 1))
            if engine == "g":
                out = grouped[:].rearrange("p (t r n4) -> p t r n4", t=PACK, n4=PACK)[:, :, places]
                in_ = z_raw[g, h][:].rearrange("p n4 (r t) -> p t r n4", t=PACK)[:, :, places]
            else:
                out = grouped[:].rearrange("p (t r n4) -> p r n4 t", t=PACK, n4=PACK)[:, places]
                in_ = z_raw[g, h][:].rearrange("p n4 (r t) -> p r n4 t", t=PACK)[:, places]
            copy(engine, out, in_)

        def zquant(g, h):
            quantise(("z", g, h), made["z_grouped", g, h])

        def wobs(b, g):
            bank = new_bank(("wobs", b, g), WOBS_BANKS[2 * g + b % 2], [P, PACK, P], F32)
            for t in range(PACK):
                nc.tensor.matmul(
                    out=bank[:, t, :],
                    lhsT=wt_diag[:, PACK * g + t, :],
                    rhs=obs_raw[g][:, t, P * b : P * (b + 1)],
                    start=True,
                    stop=True,
                )

        def by_pairs(rows):
            return rows.rearrange("p t (m2 i) -> p m2 t i", i=2)

        def words_by_pairs(words):
            return words.rearrange("p (m2 i t) -> p m2 t i", i=2, t=PACK)

        def resid(b, g):
            grouped = sbuf(("res_grouped", b // 2, g), [P, PACK * PAIR], BF16)
            nc.vector.tensor_tensor(
                out=words_by_pairs(grouped[:, PACK * P * (b % 2) : PACK * P * (b % 2 + 1)]),
                in0=by_pairs(made["wobs", b, g][:]),
                in1=by_pairs(e[g][:, :, P * b : P * (b + 1)]),
                op=ALU.add,
            )

        def rquant(q, g):
            quantise(("res", q, g), made["res_grouped", q, g])

        def moment(h, b):
            bank = new_bank(("moment", h, b), RING_BANKS[(2 * b + h) % 4], [P, PACK, P], F32)
            for t in range(PACK):
                for g in range(2):
                    z_codes, z_scales = operand(("z", g, h), slice(P * t, P * (t + 1)))
                    res_codes, res_scales = operand(("res", b // 2, g), slice(P * (b % 2), P * (b % 2 + 1)))
                    nc.tensor.matmul_mx(
                        out=bank[:, t, :],
                        lhsT=z_codes,
                        lhsT_scale=z_scales,
                        rhs=res_codes,
                        rhs_scale=res_scales,
                        start=(g == 0),
                        stop=(g == 1),
                    )

        def result_block(h, b):
            return sbuf(("result", h, b // 2), [P, PACK, PAIR], F32)[:, :, P * (b % 2) : P * (b % 2 + 1)]

        def rounded_block(h, b):
            return sbuf(("rounded", h, b // 2), [P, PACK * PAIR], BF16)[:, PACK * P * (b % 2) : PACK * P * (b % 2 + 1)]

        def drain(h, b, engine):
            copy(engine, result_block(h, b), made["moment", h, b][:])

        def roundbank(h, b, engine):
            out = rounded_block(h, b).rearrange("p (m t) -> p m t", t=PACK)
            copy(engine, out, made["moment", h, b][:].rearrange("p t m -> p m t"))

        def roundcopy(h, b, engine):
            if engine == "g":
                out = rounded_block(h, b).rearrange("p (m t) -> p m t", t=PACK)
                copy(engine, out, result_block(h, b).rearrange("p t m -> p m t"))
            else:
                copy(engine, words_by_pairs(rounded_block(h, b)), by_pairs(result_block(h, b)))

        def oquant(h, q):
            cols = slice(PAIR * q, PAIR * (q + 1))
            nc.vector.quantize_mx(
                out=out_codes[:, h, cols].bitcast(FP8X4), scales=out_scales[:, h, cols], in_=made["rounded", h, q][:]
            )

        def store(h, q):
            nc.sync.dma_start(out=out_rows[h, :, :, PAIR * q : PAIR * (q + 1)], in_=made["result", h, q][:])

        def storecodes(q):
            nc.sync.dma_start(
                out=out_words[:, :, PACK * PAIR * q : PACK * PAIR * (q + 1)].bitcast(I32),
                in_=out_codes[:, :, PAIR * q : PAIR * (q + 1)].bitcast(I32),
            )

        def storegroup(h, q):
            nc.sync.dma_start(
                out=out_words[:, h, PACK * PAIR * q : PACK * PAIR * (q + 1)].bitcast(I32),
                in_=out_codes[:, h, PAIR * q : PAIR * (q + 1)].bitcast(I32),
            )

        def storescales(d, engine):
            queue = nc.scalar if engine == "s" else nc.sync
            queue.dma_start(
                out=out_2[:, 4 * d : 4 * d + 4, :].rearrange("h r m -> r h m").bitcast(I32),
                in_=out_scales[32 * d : 32 * d + 4, :, :].bitcast(I32),
            )

        steps = dict(
            clear=clear, zero=zero, identity=identity, unit=unit, loadx=loadx, loadbeta=loadbeta,
            loadscale=loadscale, loadwt=loadwt, loadmass=loadmass, loadbs=loadbs, loadz=loadz,
            loadobs=loadobs, diag=diag, terms=terms, spread=spread, turn=turn, xpack=xpack,
            xquant=xquant, phi=phi, expo=expo, rowsum=rowsum, disc=disc, root=root, gap=gap,
            factor=factor, scale=scale, zpack=zpack, zquant=zquant, wobs=wobs, resid=resid,
            rquant=rquant, moment=moment, drain=drain, roundbank=roundbank, roundcopy=roundcopy,
            oquant=oquant, store=store, storecodes=storecodes, storegroup=storegroup,
            storescales=storescales,
        )
        for word in ORDER.split():
            head, *engine = word.split(".")
            digits = [int(ch) for ch in head if ch in "0123456789"]
            steps[head[: len(head) - len(digits)]](*digits, *engine)
